import numpy as np
import ml_dtypes


def mxq(x, axis, fmt="e4m3"):
    dtype, down = {"e4m3": (ml_dtypes.float8_e4m3fn, 7), "e5m2": (ml_dtypes.float8_e5m2, 14)}[fmt]
    v = np.moveaxis(np.asarray(x, np.float32).astype(ml_dtypes.bfloat16).astype(np.float64), axis, -1)
    blocks = v.reshape(v.shape[:-1] + (-1, 32))
    amax = np.abs(blocks).max(-1, keepdims=True)
    byte = np.maximum(np.where(amax > 0, np.frexp(amax)[1] - 1 + 127, 0) - down, 1)
    scale = np.exp2(byte - 127.0)
    codes = (blocks / scale).astype(np.float32).astype(dtype).astype(np.float64)
    return np.moveaxis((codes * scale).reshape(v.shape), -1, axis)


WIDE = False


def mx_kscale(k):
    if not WIDE:
        return np.ones(k)
    levels = np.array([10, -10, 5, -5, 0])
    if k % 512:
        return np.exp2(np.random.permutation(np.resize(levels, k // 32))).repeat(32)
    a = np.empty((k // 512, 16))
    for p in range(k // 512):
        a[p, :8] = np.random.permutation(np.resize(levels, 8))
        for g in range(8):
            far = levels[np.abs(levels - a[p, g]) >= 10]
            a[p, g + 8] = far[np.random.randint(len(far))]
    return np.exp2(a.ravel()).repeat(32)


BF16 = ml_dtypes.bfloat16


def bf(x):
    return np.asarray(x, np.float32).astype(BF16)


def f64(x):
    return np.asarray(x).astype(np.float64)


N, D, F = 512, 1024, 2048


def draw0():
    s, t = mx_kscale(D), mx_kscale(F)
    return {
        "x": bf(np.random.standard_normal((N, D)) * s),
        "w_gate": bf(np.random.standard_normal((D, F)) / np.sqrt(D) / s[:, None]),
        "b_gate": bf(0.3 * np.random.standard_normal(F)),
        "r_mag": bf(0.3 * np.random.standard_normal(F)),
        "b_mag": bf(0.3 * np.random.standard_normal(F)),
        "g_feat": bf(np.random.standard_normal(F) * t),
        "w_dec": bf(np.random.standard_normal((F, D)) / np.sqrt(F) / t[:, None]),
    }


def core(x, w_gate, b_gate, r_mag, b_mag, g_feat, w_dec):
    u = mxq(f64(x), 1, "e4m3") @ mxq(f64(w_gate), 0, "e4m3")
    pg = u + f64(b_gate)[None, :]
    pm = np.exp(f64(r_mag))[None, :] * u + f64(b_mag)[None, :]
    f = np.where(pg > 0.0, np.maximum(pm, 0.0), 0.0)
    g = f64(g_feat)[None, :]
    f_scaled = f * g
    a_scaled = np.maximum(pg, 0.0) * g
    wq = mxq(f64(w_dec), 0, "e4m3")
    xhat = mxq(f_scaled, 1, "e4m3") @ wq
    xaux = mxq(a_scaled, 1, "e4m3") @ wq
    return xhat, xaux


def e4m3fn_bytes(y):
    return np.clip(np.asarray(y, np.float64), -448.0, 448.0).astype(np.float32).astype(ml_dtypes.float8_e4m3fn).view(np.uint8)


def e4m3fn_values(b):
    return np.asarray(b, np.uint8).view(ml_dtypes.float8_e4m3fn).astype(np.float64)


def setup_inputs():
    d = draw0()
    x0 = np.asarray(d['w_gate']).astype(np.float64)
    s = (np.max(np.abs(x0), axis=(1,), keepdims=True) / 448.0).astype(np.float32)
    out = {}
    for k, v in d.items():
        if k == 'w_gate':
            out['w_gate_bytes'] = e4m3fn_bytes(x0 / s.astype(np.float64))
            out['w_gate_scale'] = s
        else:
            out[k] = v
    return out


def reference(x, w_gate_bytes, w_gate_scale, b_gate, r_mag, b_mag, g_feat, w_dec):
    return core(x, e4m3fn_values(w_gate_bytes) * w_gate_scale.astype(np.float64), b_gate, r_mag, b_mag, g_feat, w_dec)

from contextlib import ExitStack

import concourse.mybir as mybir
from concourse.masks import make_identity

N, D, F = 512, 1024, 2048
FLOPS = 2 * N * D * F * 3

F32 = mybir.dt.float32
BF16 = mybir.dt.bfloat16
U32 = mybir.dt.uint32
U8 = mybir.dt.uint8
FP8 = mybir.dt.float8_e4m3fn
FP8X4 = mybir.dt.float8_e4m3fn_x4
ALU = mybir.AluOpType
ACT = mybir.ActivationFunctionType

P = 128
FMAX = 3.4028234663852886e38


def tile_gatedsparseautoencoderwithaux_kernel(
    tc, x, w_gate_bytes, w_gate_scale, b_gate, r_mag, b_mag, g_feat, w_dec, out_0, out_1
):
    nc = tc.nc
    outs = (out_0, out_1)
    with ExitStack() as ctx:
        keep = ctx.enter_context(tc.tile_pool(name="keep", bufs=1))
        ring = ctx.enter_context(tc.tile_pool(name="ring", bufs=2))
        psum = ctx.enter_context(tc.psum_pool(name="psum", bufs=8))

        def kept(shape, dtype, name):
            return keep.tile(shape, dtype, name=name, align_bytes=64)

        def ringed(shape, dtype, name, bufs):
            return ring.tile(shape, dtype, name=name, bufs=bufs, align_bytes=64)

        def bank(shape=(P, 512), dtype=F32):
            return psum.tile(list(shape), dtype, name="bank", bufs=8)

        ctx.enter_context(tc.manual_schedule())

        ident = kept([P, P], F32, "ident")
        make_identity(nc, ident[:])
        vec = kept([P, 512], BF16, "vec")
        nc.vector.memset(vec[:], 0.0)
        warm = kept([P, 1], F32, "warm")
        nc.vector.memset(warm[:], 0.0)
        sc = kept([P, 2, 4], F32, "sc")
        for v, src in enumerate((b_gate, r_mag, b_mag, g_feat)):
            nc.scalar.dma_start(out=vec[4 * v : 4 * v + 4, :], in_=src.rearrange("(g c) -> g c", g=4))
        nc.scalar.dma_start(out=sc[:], in_=w_gate_scale.rearrange("(g p t) o -> p g (t o)", p=P, t=4))
        warm2 = kept([P, 1], F32, "warm2")
        nc.scalar.activation(out=warm2[:], in_=warm[:], func=ACT.Exp)

        wbytes = {}

        def load_bytes(g0, ng):
            for kp in range(2):
                t = kept([P, 4, 512 * ng], U8, "wbytes%d%d" % (g0, kp))
                nc.sync.dma_start(
                    out=t[:],
                    in_=w_gate_bytes[512 * kp : 512 * kp + 512, 512 * g0 : 512 * (g0 + ng)].rearrange(
                        "(p j) n -> p j n", j=4
                    ),
                )
                for g in range(ng):
                    wbytes[g0 + g, kp] = (t, 512 * g)

        load_bytes(0, 1)
        xs = []
        for m in range(4):
            t = kept([P, D], BF16, "x%d" % m)
            nc.sync.dma_start(out=t[:], in_=x[P * m : P * m + P, :])
            xs.append(t)
        load_bytes(1, 1)
        load_bytes(2, 2)
        wd_raw = {}
        for h in range(2):
            for p in range(4):
                t = ringed([P, 4, 512], BF16, "wd_raw", 6)
                nc.sync.dma_start(
                    out=t[:],
                    in_=w_dec[512 * p : 512 * p + 512, 512 * h : 512 * h + 512].rearrange(
                        "(p j) n -> p j n", j=4
                    ),
                )
                wd_raw[h, p] = t

        wide, wgrp, wq, ws = {}, {}, {}, {}

        def widen(g, kp, j, eng):
            if (g, kp) not in wide:
                wide[g, kp] = ringed([P, 4, 512], BF16, "wide", 4)
            raw, c0 = wbytes[g, kp]
            src = raw[:, j, c0 : c0 + 512].bitcast(FP8)
            dst = wide[g, kp][:, j, :]
            if eng == "s":
                nc.scalar.activation(out=dst, in_=src, func=ACT.Copy, scale=sc[:, kp, j : j + 1])
            else:
                nc.vector.tensor_scalar(
                    out=dst, in0=src, scalar1=sc[:, kp, j : j + 1], scalar2=None, op0=ALU.mult
                )

        def ilv_w(g, kp):
            t = ringed([P, 2048], BF16, "wgrp", 3)
            wgrp[g, kp] = t
            nc.vector.tensor_copy(
                out=t[:].rearrange("p (t c i j) -> p t c j i", t=4, i=4, j=4),
                in_=wide[g, kp][:].rearrange("p j (c i t) -> p t c j i", i=4, t=4),
            )

        def quant(src, name):
            width = src.shape[1] // 4
            codes = kept([P, width], U32, name + "_q")
            scales = kept([P, width], U8, name + "_s")
            nc.vector.quantize_mx(out=codes[:].bitcast(FP8X4), scales=scales[:], in_=src)
            return codes, scales

        def quant_w(g, kp):
            wq[g, kp] = quant(wgrp[g, kp][:], "w%d%d" % (g, kp))

        xgrp = kept([P, 2, 512, 4], BF16, "xgrp")
        xbank = {}

        def x_turn(m):
            b = bank()
            words = xs[m][:].bitcast(F32)
            for g in range(2):
                for u in range(2):
                    c = 128 * (2 * g + u)
                    nc.tensor.transpose(
                        b[:, c : c + 128], words[:, 256 * g + u : 256 * (g + 1) : 2], ident[:]
                    )
            xbank[m] = b

        def x_out(m, eng):
            dst = xgrp[:, :, P * m : P * m + P, :].rearrange("p g r t -> p g (r t)").bitcast(F32)
            dst = dst.rearrange("p g (r u) -> p g r u", u=2)
            src = xbank[m][:].rearrange("p (g u r) -> p g r u", g=2, u=2)
            if eng == "s":
                nc.scalar.copy(out=dst, in_=src)
            else:
                nc.vector.tensor_copy(out=dst, in_=src)

        xq = {}

        def quant_x(kp):
            xq[kp] = quant(xgrp[:, kp, :, :].rearrange("p r t -> p (r t)"), "x%d" % kp)

        ub = {}

        def stage1(g):
            for t in range(4):
                b = bank()
                for kp in range(2):
                    cols = slice(128 * t, 128 * t + 128)
                    nc.tensor.matmul_mx(
                        out=b[:],
                        lhsT=wq[g, kp][0][:, cols].bitcast(FP8X4),
                        lhsT_scale=wq[g, kp][1][:, cols],
                        rhs=xq[kp][0][:].bitcast(FP8X4),
                        rhs_scale=xq[kp][1][:],
                        start=(kp == 0),
                        stop=(kp == 1),
                    )
                ub[g, t] = b

        prm = {}
        az = {}

        def affine(g, ts=(0, 1, 2, 3)):
            if g not in az:
                az[g] = ringed([P, 4, 2, 512], BF16, "az", 3)
            for t in ts:
                col = (slice(None), t, slice(g, g + 1))
                nc.scalar.activation(
                    out=az[g][:, t, 0, :], in_=ub[g, t][:], func=ACT.Identity, bias=prm["gb"][col], scale=prm["g"][col]
                )
                nc.scalar.activation(
                    out=az[g][:, t, 1, :], in_=ub[g, t][:], func=ACT.Identity, bias=prm["gm"][col], scale=prm["ge"][col]
                )

        def clamp(g):
            for t in range(4):
                col = (slice(None), t, slice(g, g + 1))
                v = az[g][:, t, :, :].rearrange("p a n -> p (a n)")
                nc.vector.tensor_scalar(
                    out=v, in0=v, scalar1=prm["lo"][col], scalar2=prm["hi"][col], op0=ALU.max, op1=ALU.min
                )

        agrp, fgrp = {}, {}

        def ilv_a(g):
            t = ringed([P, 512, 4], BF16, "agrp", 2)
            agrp[g] = t
            nc.vector.tensor_copy(
                out=t[:].rearrange("p (c i) t -> p c t i", i=4),
                in_=az[g][:, :, 0, :].rearrange("p t (c i) -> p c t i", i=4),
            )

        def gate_f(g):
            t = ringed([P, 512, 4], BF16, "fgrp", 2)
            fgrp[g] = t
            nc.vector.scalar_tensor_tensor(
                out=t[:],
                in0=agrp[g][:],
                scalar=0.0,
                in1=az[g][:, :, 1, :].rearrange("p t n -> p n t"),
                op0=ALU.not_equal,
                op1=ALU.mult,
            )

        afq = {}

        def quant_a(g):
            afq[0, g] = quant(agrp[g][:].rearrange("p n t -> p (n t)"), "a%d" % g)

        def quant_f(g):
            afq[1, g] = quant(fgrp[g][:].rearrange("p n t -> p (n t)"), "f%d" % g)

        wdgrp, wdq = {}, {}

        def ilv_d(h, p, eng="v"):
            t = ringed([P, 512, 4], BF16, "wdgrp", 3)
            wdgrp[h, p] = t
            dst = t[:].rearrange("p (c i) t -> p c t i", i=4)
            src = wd_raw[h, p][:].rearrange("p t (c i) -> p c t i", i=4)
            if eng == "s":
                nc.scalar.copy(out=dst, in_=src)
            else:
                nc.vector.tensor_copy(out=dst, in_=src)

        def quant_d(h, p):
            wdq[h, p] = quant(wdgrp[h, p][:].rearrange("p n t -> p (n t)"), "d%d%d" % (h, p))

        acc = {}

        def stage2(which, h, p, ms=(0, 1, 2, 3)):
            for m in ms:
                if p == 0:
                    acc[which, h, m] = bank()
                cols = slice(128 * m, 128 * m + 128)
                nc.tensor.matmul_mx(
                    out=acc[which, h, m][:],
                    lhsT=afq[which, p][0][:, cols].bitcast(FP8X4),
                    lhsT_scale=afq[which, p][1][:, cols],
                    rhs=wdq[h, p][0][:].bitcast(FP8X4),
                    rhs_scale=wdq[h, p][1][:],
                    start=(p == 0),
                    stop=(p == 3),
                )

        def emit(which, h, m, eng):
            t = ringed([P, 512], F32, "res", 8)
            if eng == "s":
                nc.scalar.copy(out=t[:], in_=acc[which, h, m][:])
            else:
                nc.vector.tensor_copy(out=t[:], in_=acc[which, h, m][:])
            nc.sync.dma_start(
                out=outs[1 - which][P * m : P * m + P, 512 * h : 512 * h + 512], in_=t[:]
            )

        vecf = kept([P, 4, P], F32, "vecf")
        nc.vector.tensor_copy(out=vecf[:], in_=vec[:].rearrange("p (m t) -> p t m", t=4))
        vb = bank()
        for t in range(4):
            nc.tensor.transpose(vb[:, 128 * t : 128 * t + 128], vecf[:, t, :], ident[:])

        widen(0, 0, 0, "s")
        for j in (1, 2, 3):
            widen(0, 0, j, "v")
        widen(0, 1, 0, "s")
        widen(0, 1, 1, "s")
        widen(0, 1, 2, "v")
        widen(0, 1, 3, "v")

        raw_prm = kept([P, 4, 16], F32, "raw_prm")
        nc.vector.tensor_copy(
            out=raw_prm[:], in_=vb[:].rearrange("p (t r) -> p t r", t=4)[:, :, 0:16]
        )
        b_c, r_c, m_c, g_c = (raw_prm[:, :, 4 * v : 4 * v + 4] for v in range(4))
        for nm in ("e", "gb", "ge", "gm", "lo", "hi"):
            prm[nm] = kept([P, 4, 4], F32, "prm_" + nm)
        prm["g"] = g_c
        nc.scalar.activation(out=prm["e"][:], in_=r_c, func=ACT.Exp)
        nc.gpsimd.tensor_tensor(out=prm["gb"][:], in0=g_c, in1=b_c, op=ALU.mult)
        nc.gpsimd.tensor_tensor(out=prm["gm"][:], in0=g_c, in1=m_c, op=ALU.mult)
        nc.gpsimd.tensor_scalar(
            out=prm["lo"][:], in0=g_c, scalar1=0.0, scalar2=-FMAX, op0=ALU.is_lt, op1=ALU.mult
        )
        nc.gpsimd.tensor_scalar(
            out=prm["hi"][:], in0=g_c, scalar1=0.0, scalar2=FMAX, op0=ALU.is_ge, op1=ALU.mult
        )
        nc.gpsimd.tensor_tensor(out=prm["ge"][:], in0=g_c, in1=prm["e"][:], op=ALU.mult)

        for m in range(4):
            x_turn(m)
        x_out(0, "s")
        x_out(1, "s")
        ilv_w(0, 0)
        x_out(2, "v")
        ilv_w(0, 1)
        x_out(3, "v")
        quant_w(0, 0)
        quant_w(0, 1)
        quant_x(0)
        quant_x(1)
        stage1(0)
        for kp in range(2):
            for j in range(4):
                widen(1, kp, j, "s")
        ilv_d(0, 0)
        affine(0)
        ilv_w(1, 0)
        ilv_w(1, 1)
        quant_d(0, 0)
        quant_w(1, 0)
        quant_w(1, 1)
        stage1(1)

        for g in (0, 1):
            for kp in range(2):
                for j in range(4):
                    widen(g + 2, kp, j, "s")
            affine(g + 1)
            ilv_d(0, g + 1)
            clamp(g)
            quant_d(0, g + 1)
            ilv_a(g)
            ilv_w(g + 2, 0)
            gate_f(g)
            quant_a(g)
            ilv_w(g + 2, 1)
            quant_f(g)
            quant_w(g + 2, 0)
            quant_w(g + 2, 1)
            stage1(g + 2)

        affine(3)
        ilv_d(1, 0, "s")
        ilv_d(0, 3)
        clamp(2)
        quant_d(0, 3)
        ilv_a(2)
        stage2(0, 0, 0)
        stage2(0, 0, 1)
        clamp(3)
        gate_f(2)
        quant_a(2)
        stage2(0, 0, 2)
        ilv_a(3)
        quant_f(2)
        quant_d(1, 0)
        ilv_d(1, 1, "s")
        quant_a(3)
        stage2(0, 0, 3)
        stage2(1, 0, 0)
        stage2(1, 0, 1)
        stage2(1, 0, 2)
        gate_f(3)
        quant_d(1, 1)
        quant_f(3)
        stage2(1, 0, 3)
        ilv_d(1, 2, "s")
        for m in range(4):
            emit(0, 0, m, "s")
        ilv_d(1, 3)
        quant_d(1, 2)
        quant_d(1, 3)
        emit(1, 0, 0, "v")
        emit(1, 0, 1, "s")
        emit(1, 0, 2, "v")
        emit(1, 0, 3, "s")
        for p in range(4):
            stage2(0, 1, p)
        for p in range(4):
            stage2(1, 1, p)
        for which in range(2):
            for m in range(4):
                emit(which, 1, m, "v" if m % 2 == 0 else "s")
